import numpy as np
import ml_dtypes


def mxq(x, axis, fmt="e4m3"):
    dtype, down = {"e4m3": (ml_dtypes.float8_e4m3fn, 7), "e5m2": (ml_dtypes.float8_e5m2, 14)}[fmt]
    v = np.moveaxis(np.asarray(x, np.float32).astype(ml_dtypes.bfloat16).astype(np.float64), axis, -1)
    blocks = v.reshape(v.shape[:-1] + (-1, 32))
    amax = np.abs(blocks).max(-1, keepdims=True)
    byte = np.maximum(np.where(amax > 0, np.frexp(amax)[1] - 1 + 127, 0) - down, 1)
    scale = np.exp2(byte - 127.0)
    codes = (blocks / scale).astype(np.float32).astype(dtype).astype(np.float64)
    return np.moveaxis((codes * scale).reshape(v.shape), -1, axis)


WIDE = False


def mx_kscale(k):
    if not WIDE:
        return np.ones(k)
    levels = np.array([10, -10, 5, -5, 0])
    if k % 512:
        return np.exp2(np.random.permutation(np.resize(levels, k // 32))).repeat(32)
    a = np.empty((k // 512, 16))
    for p in range(k // 512):
        a[p, :8] = np.random.permutation(np.resize(levels, 8))
        for g in range(8):
            far = levels[np.abs(levels - a[p, g]) >= 10]
            a[p, g + 8] = far[np.random.randint(len(far))]
    return np.exp2(a.ravel()).repeat(32)


def f64(x):
    return np.asarray(x).astype(np.float64)


def striped(idx):
    return np.tile(idx.reshape(-1, 16).T, (8, 1)).astype(np.uint16)


def unstriped(offs):
    return offs[:16].T.reshape(-1).astype(np.int64)


def pack_weight(w):
    k, n = w.shape
    w = f64(np.asarray(w, np.float32).astype(ml_dtypes.bfloat16)).reshape(k // 32, 32, n)
    amax = np.abs(w).max(1)
    byte = np.clip(np.where(amax > 0, np.frexp(amax)[1] - 1 + 127 - 7, 1), 1, 254)
    scaled = (w * np.exp2(127.0 - byte)[:, None, :]).reshape(k, n).astype(np.float32)
    words = np.ascontiguousarray(scaled.reshape(k // 512, 128, 4, n).transpose(0, 1, 3, 2)).astype(ml_dtypes.float8_e4m3fn).view(np.uint8)
    return words, np.ascontiguousarray(byte.astype(np.uint8).reshape(k // 512, 16, n))


def unpack_weight(words, scales):
    g, p, n, _ = words.shape
    vals = np.ascontiguousarray(words).view(ml_dtypes.float8_e4m3fn).astype(np.float64) * np.repeat(np.exp2(scales.astype(np.float64) - 127.0), 8, axis=1)[..., None]
    return vals.transpose(0, 1, 3, 2).reshape(g * 512, n)

def planes(y):
    n, m = y.shape
    v = y.astype(np.float32).astype(ml_dtypes.bfloat16).astype(np.float64).reshape(n // 32, 32, m)
    top = np.abs(v).max(1)
    byte = np.clip(np.where(top > 0, np.frexp(top)[1] - 1 + 127 - 7, 1), 1, 254)
    codes = (v * np.exp2(127.0 - byte)[:, None, :]).reshape(n, m).astype(np.float32).astype(ml_dtypes.float8_e4m3fn).view(np.uint8)
    words = codes.reshape(n // 512, 128, 4, m).transpose(0, 1, 3, 2)
    return np.ascontiguousarray(words), np.ascontiguousarray(byte.astype(np.uint8).reshape(n // 512, 16, m))


K, T, S, H, C = 512, 2048, 256, 512, 512


def setup_inputs():
    n = np.random.standard_normal
    s = mx_kscale(K)[:, None]
    packed_xT = pack_weight(n((K, T)) * s)
    packed_w1 = pack_weight(n((K, H)) / np.sqrt(K) / s)
    return {
        "x_words": packed_xT[0],
        "x_scales": packed_xT[1],
        "w1_words": packed_w1[0],
        "w1_scales": packed_w1[1],
        "gs": (np.random.uniform(0.5, 1.5, (K, 1)) / s).astype(np.float32),
        "offs": striped(np.random.permutation(T)[:S]),
        "n1": striped(np.random.permutation(S)),
        "n2": striped(np.random.permutation(S)),
        "ca": striped(np.random.permutation(T)[:C]),
        "cb": striped(np.random.permutation(T)[:C]),
        "n3": striped(np.random.permutation(S)),
        "n4": striped(np.random.permutation(S)),
        "n5": striped(np.random.permutation(S)),
        "n6": striped(np.random.permutation(S)),
    }


def reference(x_words, x_scales, w1_words, w1_scales, gs, offs, n1, n2, ca, cb, n3, n4, n5, n6):
    x_ca = unpack_weight(x_words, x_scales)[:, unstriped(ca)]
    xq = unpack_weight(x_words, x_scales)[:, unstriped(offs)]
    y = unpack_weight(w1_words, w1_scales).T @ xq
    st = np.maximum(y, y[:, unstriped(n1)])
    z = f64(gs) * (st[:, unstriped(n2)] - (0.5 * y))
    zq = mxq(z, 0, "e4m3")
    a = 0.0625 * (x_ca.T @ zq)
    x_cb = unpack_weight(x_words, x_scales)[:, unstriped(cb)]
    b = 0.0625 * (x_cb.T @ zq)
    out_0 = np.maximum(a[:, unstriped(n3)] + b[:, unstriped(n5)], a[:, unstriped(n4)] + b[:, unstriped(n6)])
    return (out_0,) + planes(out_0)

@@ -1,0 +1,226 @@
+from contextlib import ExitStack
+
+import concourse.mybir as mybir
+
+K, T, S, H, C = 512, 2048, 256, 512, 512
+FLOPS = 2 * K * S * (H + 2 * C)
+
+F32 = mybir.dt.float32
+BF16 = mybir.dt.bfloat16
+I32 = mybir.dt.int32
+U32 = mybir.dt.uint32
+U16 = mybir.dt.uint16
+U8 = mybir.dt.uint8
+FP8X4 = mybir.dt.float8_e4m3fn_x4
+ALU = mybir.AluOpType
+COPY = mybir.ActivationFunctionType.Copy
+
+P = 128
+PACK = 4
+HALF = S // 2
+SPARE = 16
+PER_COL = 16
+
+
+def tile_picked_ccmppathbhopb_none_po_kernel(
+    tc, x_words, x_scales, w1_words, w1_scales, gs, offs, n1, n2, ca, cb, n3, n4, n5, n6, out_0, out_1, out_2
+):
+    nc = tc.nc
+    with ExitStack() as ctx:
+        sb = ctx.enter_context(tc.tile_pool(name="sb", bufs=1))
+        ps = ctx.enter_context(tc.psum_pool(name="ps", bufs=1))
+
+        def load_list(src, name):
+            lst = sb.tile(list(src.shape), U16, name=name)
+            nc.sync.dma_start(lst[:], src)
+            return lst
+
+        def load_words(src, cols, name):
+            words = sb.tile([P, cols], U32, name=name, align_bytes=64)
+            nc.sync.dma_start(words[:].bitcast(I32), src[0].rearrange("p n t -> p (n t)").bitcast(I32))
+            return words
+
+        def load_scale_rows(plane, src):
+            for q in range(4):
+                nc.sync.dma_start(plane[32 * q : 32 * q + 4, :].bitcast(I32), src[0, 4 * q : 4 * q + 4, :].bitcast(I32))
+
+        def half_cols(h):
+            return slice(h * HALF, (h + 1) * HALF)
+
+        def half_list(lst, h):
+            return lst[:, h * HALF // PER_COL : (h + 1) * HALF // PER_COL]
+
+        x_plane = sb.tile([P, T], U8, name="x_plane", align_bytes=64)
+        nc.vector.memset(x_plane[:].bitcast(I32), 0)
+        w_plane = sb.tile([P, H], U8, name="w_plane", align_bytes=64)
+        nc.vector.memset(w_plane[:].bitcast(I32), 0)
+        gs_sb = sb.tile([P, PACK], F32, name="gs_sb")
+        y_sb = [sb.tile([P, S + SPARE], F32, name="y_sb%d" % t) for t in range(PACK)]
+        for t in range(PACK):
+            nc.vector.memset(y_sb[t][:, S:], 0.0)
+
+        w_words = load_words(w1_words, H, "w_words")
+        load_scale_rows(x_plane, x_scales)
+        offs_l = load_list(offs, "offs_l")
+        ca_l = load_list(ca, "ca_l")
+        load_scale_rows(w_plane, w1_scales)
+        cb_l = load_list(cb, "cb_l")
+        x_sb = load_words(x_words, T, "x_sb")
+        n1_l = load_list(n1, "n1_l")
+        nc.sync.dma_start(gs_sb[:], gs.rearrange("(p t) o -> p (t o)", t=PACK))
+        n2_l = load_list(n2, "n2_l")
+        n3_l = load_list(n3, "n3_l")
+        n5_l = load_list(n5, "n5_l")
+        n4_l = load_list(n4, "n4_l")
+        n6_l = load_list(n6, "n6_l")
+
+        neg_half_gs = sb.tile([P, PACK], F32, name="neg_half_gs")
+        nc.scalar.activation(neg_half_gs[:], gs_sb[:], COPY, scale=-0.5)
+
+        def deal_bytes(raw, name):
+            dealt = sb.tile([P, C], U8, name=name, align_bytes=64)
+            nc.vector.tensor_copy(
+                dealt[:].rearrange("p (t m) -> p t m", t=PACK), raw[:].rearrange("p (m t) -> p t m", t=PACK)
+            )
+            return dealt
+
+        def gather_bytes(lst, cols, name, tag):
+            got = sb.tile([P, cols], U8, name=name, tag=tag, align_bytes=64)
+            nc.vector.tensor_copy(got[:], x_plane[:].indirect(lst[:]))
+            return got
+
+        def gather_words_dealt(lst, name):
+            got = sb.tile([P, C], U32, name=name, align_bytes=64)
+            nc.vector.tensor_copy(got[:].rearrange("p (t m) -> p m t", t=PACK), x_sb[:].indirect(lst[:]))
+            return got
+
+        w_dealt = sb.tile([P, H], U32, name="w_dealt", align_bytes=64)
+        nc.vector.tensor_copy(
+            w_dealt[:].rearrange("p (t c i) -> p c t i", t=PACK, i=4),
+            w_words[:].rearrange("p (c i t) -> p c t i", t=PACK, i=4),
+        )
+        xq_scales = gather_bytes(offs_l, S, "xq_scales", "picked_bytes")
+        ca_raw = gather_bytes(ca_l, C, "ca_raw", "ca_raw")
+        w_scales = deal_bytes(w_plane, "w_scales")
+        ca_scales = deal_bytes(ca_raw, "ca_scales")
+        cb_raw = gather_bytes(cb_l, C, "cb_raw", "cb_raw")
+        cb_scales = deal_bytes(cb_raw, "cb_scales")
+        xq_words = sb.tile([P, S], U32, name="xq_words", align_bytes=64)
+        nc.vector.tensor_copy(xq_words[:], x_sb[:].indirect(offs_l[:]))
+
+        def product(out, words, scales, t, rhs_words, rhs_scales):
+            cols = slice(t * P, (t + 1) * P)
+            nc.tensor.matmul_mx(
+                out=out,
+                lhsT=words[:, cols].bitcast(FP8X4),
+                lhsT_scale=scales[:, cols],
+                rhs=rhs_words.bitcast(FP8X4),
+                rhs_scale=rhs_scales,
+                start=True,
+                stop=True,
+            )
+
+        y_ps = [ps.tile([P, S], F32, name="y_ps%d" % t, tag="bank%d" % t) for t in range(PACK)]
+        for t in range(PACK):
+            product(y_ps[t][:], w_dealt, w_scales, t, xq_words[:], xq_scales[:])
+
+        ca_words = gather_words_dealt(ca_l, "ca_words")
+        cb_words = gather_words_dealt(cb_l, "cb_words")
+
+        y_n1 = [sb.tile([P, S], F32, name="y_n1_%d" % t) for t in range(PACK)]
+        st = [sb.tile([P, S], F32, name="st%d" % t) for t in range(PACK)]
+        own = [sb.tile([P, S], F32, name="own%d" % t) for t in range(PACK)]
+        for t in range(PACK):
+            nc.scalar.activation(y_sb[t][:, :S], y_ps[t][:], COPY)
+            nc.scalar.activation(y_n1[t][:], y_sb[t][:].indirect(n1_l[:]), COPY)
+        for t in range(PACK):
+            nc.vector.tensor_tensor(st[t][:], y_n1[t][:], y_sb[t][:, :S], ALU.max)
+            nc.vector.tensor_scalar(own[t][:], y_sb[t][:, :S], neg_half_gs[:, t : t + 1], None, ALU.mult)
+
+        st_n2 = sb.tile([P, PACK, S], F32, name="st_n2")
+        z_f32 = sb.tile([P, PACK, S], F32, name="z_f32")
+        z_bf = sb.tile([P, S, PACK], BF16, name="z_bf", align_bytes=64)
+        z_words = sb.tile([P, S], U32, name="z_words", align_bytes=64)
+        z_scales = sb.tile([P, S], U8, name="z_scales", align_bytes=64)
+
+        def interleave(engine_copy, dst, src, h):
+            engine_copy(
+                dst[:, half_cols(h), :].rearrange("p (c i) t -> p c t i", i=4),
+                src[:, :, half_cols(h)].rearrange("p t (c i) -> p c t i", i=4),
+            )
+
+        def quantise(words, scales, src, h):
+            nc.vector.quantize_mx(
+                out=words[:, half_cols(h)].bitcast(FP8X4),
+                scales=scales[:, half_cols(h)],
+                in_=src[:, half_cols(h), :].rearrange("p j t -> p (j t)"),
+            )
+
+        a_sb = [sb.tile([P, S], F32, name="a_sb%d" % t) for t in range(PACK)]
+        b_sb = [sb.tile([P, S], F32, name="b_sb%d" % t) for t in range(PACK)]
+
+        for h in range(2):
+            for t in range(PACK):
+                nc.scalar.activation(st_n2[:, t, half_cols(h)], st[t][:].indirect(half_list(n2_l, h)), COPY)
+                nc.vector.scalar_tensor_tensor(
+                    z_f32[:, t, half_cols(h)],
+                    st_n2[:, t, half_cols(h)],
+                    gs_sb[:, t : t + 1],
+                    own[t][:, half_cols(h)],
+                    ALU.mult,
+                    ALU.add,
+                )
+            interleave(nc.vector.tensor_copy, z_bf, z_f32, h)
+            quantise(z_words, z_scales, z_bf, h)
+
+        first_a = ps.tile([P, PACK, HALF], F32, name="first_a")
+        first_b = ps.tile([P, PACK, HALF], F32, name="first_b")
+        for t in range(PACK):
+            product(first_a[:, t, :], ca_words, ca_scales, t, z_words[:, half_cols(0)], z_scales[:, half_cols(0)])
+        for t in range(PACK):
+            product(first_b[:, t, :], cb_words, cb_scales, t, z_words[:, half_cols(0)], z_scales[:, half_cols(0)])
+        for t in range(PACK):
+            nc.scalar.activation(a_sb[t][:, half_cols(0)], first_a[:, t, :], COPY, scale=0.0625)
+        for t in range(PACK):
+            nc.scalar.activation(b_sb[t][:, half_cols(0)], first_b[:, t, :], COPY, scale=0.0625)
+
+        a_n3 = sb.tile([P, PACK, S], F32, name="a_n3")
+        a_n4 = sb.tile([P, PACK, S], F32, name="a_n4")
+        sum35 = sb.tile([P, PACK, S], F32, name="sum35")
+        sum46 = sb.tile([P, PACK, S], F32, name="sum46")
+        o_f32 = sb.tile([P, PACK, S], F32, name="o_f32")
+        o_bf = sb.tile([P, S, PACK], BF16, name="o_bf", align_bytes=64)
+        o_words = sb.tile([P, S], U32, name="o_words", align_bytes=64)
+        o_scales = sb.tile([P, S], U8, name="o_scales", align_bytes=64)
+        out_rows = out_0.rearrange("(p t) j -> p t j", t=PACK)
+        out_words = out_1[0].rearrange("p n t -> p (n t)").bitcast(I32)
+
+        for h in range(2):
+            cols = half_cols(h)
+            for t in range(PACK):
+                if h == 0:
+                    second_a = ps.tile([P, HALF], F32, name="second_a", tag="bank%d" % t)
+                    second_b = ps.tile([P, HALF], F32, name="second_b", tag="late_b%d" % (t % 2))
+                    product(second_a[:], ca_words, ca_scales, t, z_words[:, half_cols(1)], z_scales[:, half_cols(1)])
+                    product(second_b[:], cb_words, cb_scales, t, z_words[:, half_cols(1)], z_scales[:, half_cols(1)])
+                    nc.scalar.activation(a_sb[t][:, half_cols(1)], second_a[:], COPY, scale=0.0625)
+                    if t < 2:
+                        nc.vector.tensor_scalar(b_sb[t][:, half_cols(1)], second_b[:], 0.0625, None, ALU.mult)
+                    else:
+                        nc.scalar.activation(b_sb[t][:, half_cols(1)], second_b[:], COPY, scale=0.0625)
+                nc.scalar.activation(a_n3[:, t, cols], a_sb[t][:].indirect(half_list(n3_l, h)), COPY)
+                nc.scalar.activation(a_n4[:, t, cols], a_sb[t][:].indirect(half_list(n4_l, h)), COPY)
+                nc.vector.tensor_tensor(
+                    sum35[:, t, cols], b_sb[t][:].indirect(half_list(n5_l, h)), a_n3[:, t, cols], ALU.add
+                )
+                nc.vector.tensor_tensor(
+                    sum46[:, t, cols], b_sb[t][:].indirect(half_list(n6_l, h)), a_n4[:, t, cols], ALU.add
+                )
+                nc.vector.tensor_tensor(o_f32[:, t, cols], sum35[:, t, cols], sum46[:, t, cols], ALU.max)
+            nc.sync.dma_start(out_rows[:, :, cols], o_f32[:, :, cols])
+            interleave(nc.vector.tensor_copy, o_bf, o_f32, h)
+            quantise(o_words, o_scales, o_bf, h)
+            nc.sync.dma_start(out_words[:, cols], o_words[:, cols].bitcast(I32))
+        for q in range(4):
+            queue = nc.scalar if q % 2 == 0 else nc.sync
+            queue.dma_start(out_2[0, 4 * q : 4 * q + 4, :].bitcast(I32), o_scales[32 * q : 32 * q + 4, :].bitcast(I32))

@@ -20,6 +20,7 @@ PACK = 4
 HALF = S // 2
 SPARE = 16
 PER_COL = 16
+ON_VECTOR = 176
 
 
 def tile_picked_ccmppathbhopb_none_po_kernel(
@@ -28,6 +29,7 @@ def tile_picked_ccmppathbhopb_none_po_kernel(
     nc = tc.nc
     with ExitStack() as ctx:
         sb = ctx.enter_context(tc.tile_pool(name="sb", bufs=1))
+        shared = ctx.enter_context(tc.tile_pool(name="shared", bufs=1))
         ps = ctx.enter_context(tc.psum_pool(name="ps", bufs=1))
 
         def load_list(src, name):
@@ -35,9 +37,9 @@ def tile_picked_ccmppathbhopb_none_po_kernel(
             nc.sync.dma_start(lst[:], src)
             return lst
 
-        def load_words(src, cols, name):
+        def load_words(queue, src, cols, name):
             words = sb.tile([P, cols], U32, name=name, align_bytes=64)
-            nc.sync.dma_start(words[:].bitcast(I32), src[0].rearrange("p n t -> p (n t)").bitcast(I32))
+            queue.dma_start(words[:].bitcast(I32), src[0].rearrange("p n t -> p (n t)").bitcast(I32))
             return words
 
         def load_scale_rows(plane, src):
@@ -50,35 +52,44 @@ def tile_picked_ccmppathbhopb_none_po_kernel(
         def half_list(lst, h):
             return lst[:, h * HALF // PER_COL : (h + 1) * HALF // PER_COL]
 
-        x_plane = sb.tile([P, T], U8, name="x_plane", align_bytes=64)
-        nc.vector.memset(x_plane[:].bitcast(I32), 0)
-        w_plane = sb.tile([P, H], U8, name="w_plane", align_bytes=64)
-        nc.vector.memset(w_plane[:].bitcast(I32), 0)
-        gs_sb = sb.tile([P, PACK], F32, name="gs_sb")
-        y_sb = [sb.tile([P, S + SPARE], F32, name="y_sb%d" % t) for t in range(PACK)]
-        for t in range(PACK):
-            nc.vector.memset(y_sb[t][:, S:], 0.0)
+        def plane(t, planes=1):
+            return slice(t * S, (t + planes) * S)
 
-        w_words = load_words(w1_words, H, "w_words")
-        load_scale_rows(x_plane, x_scales)
+        x_plane = sb.tile([P, T], U8, name="x_plane", align_bytes=64)
+        nc.vector.memset(x_plane[:, : T // 2].bitcast(I32), 0)
+        nc.gpsimd.memset(x_plane[:, T // 2 :].bitcast(I32), 0)
+        w_plane = shared.tile([P, H], U8, name="w_plane", offset=4 * C - H // 2, align_bytes=64)
+        nc.vector.memset(w_plane[:].bitcast(I32), 0)
+
+        def window(name):
+            win = sb.tile([P, S + SPARE], F32, name=name)
+            nc.gpsimd.memset(win[:, S:], 0.0)
+            return win
+
+        y_neg = sb.tile([P, (PACK + 1) * S], F32, name="y_neg")
+        nc.vector.memset(y_neg[:, plane(PACK)], 0.0)
+        st = [window("st%d" % t) for t in range(PACK)]
+        a_sb = [window("a_sb%d" % t) for t in range(PACK)]
+        b_sb = [window("b_sb%d" % t) for t in range(PACK)]
+
         offs_l = load_list(offs, "offs_l")
+        w_words = load_words(nc.scalar, w1_words, H, "w_words")
+        load_scale_rows(x_plane, x_scales)
         ca_l = load_list(ca, "ca_l")
+        x_sb = load_words(nc.sync, x_words, T, "x_sb")
         load_scale_rows(w_plane, w1_scales)
-        cb_l = load_list(cb, "cb_l")
-        x_sb = load_words(x_words, T, "x_sb")
         n1_l = load_list(n1, "n1_l")
-        nc.sync.dma_start(gs_sb[:], gs.rearrange("(p t) o -> p (t o)", t=PACK))
+        cb_l = load_list(cb, "cb_l")
         n2_l = load_list(n2, "n2_l")
+        gs_sb = sb.tile([P, PACK], F32, name="gs_sb")
+        nc.sync.dma_start(gs_sb[:], gs.rearrange("(p t) o -> p (t o)", t=PACK))
         n3_l = load_list(n3, "n3_l")
         n5_l = load_list(n5, "n5_l")
         n4_l = load_list(n4, "n4_l")
         n6_l = load_list(n6, "n6_l")
 
-        neg_half_gs = sb.tile([P, PACK], F32, name="neg_half_gs")
-        nc.scalar.activation(neg_half_gs[:], gs_sb[:], COPY, scale=-0.5)
-
-        def deal_bytes(raw, name):
-            dealt = sb.tile([P, C], U8, name=name, align_bytes=64)
+        def deal_bytes(raw, name, tag):
+            dealt = sb.tile([P, C], U8, name=name, tag=tag, align_bytes=64)
             nc.vector.tensor_copy(
                 dealt[:].rearrange("p (t m) -> p t m", t=PACK), raw[:].rearrange("p (m t) -> p t m", t=PACK)
             )
@@ -89,24 +100,10 @@ def tile_picked_ccmppathbhopb_none_po_kernel(
             nc.vector.tensor_copy(got[:], x_plane[:].indirect(lst[:]))
             return got
 
-        def gather_words_dealt(lst, name):
-            got = sb.tile([P, C], U32, name=name, align_bytes=64)
+        def gather_words_dealt(lst, name, tag):
+            got = sb.tile([P, C], U32, name=name, tag=tag, align_bytes=64)
             nc.vector.tensor_copy(got[:].rearrange("p (t m) -> p m t", t=PACK), x_sb[:].indirect(lst[:]))
             return got
-
-        w_dealt = sb.tile([P, H], U32, name="w_dealt", align_bytes=64)
-        nc.vector.tensor_copy(
-            w_dealt[:].rearrange("p (t c i) -> p c t i", t=PACK, i=4),
-            w_words[:].rearrange("p (c i t) -> p c t i", t=PACK, i=4),
-        )
-        xq_scales = gather_bytes(offs_l, S, "xq_scales", "picked_bytes")
-        ca_raw = gather_bytes(ca_l, C, "ca_raw", "ca_raw")
-        w_scales = deal_bytes(w_plane, "w_scales")
-        ca_scales = deal_bytes(ca_raw, "ca_scales")
-        cb_raw = gather_bytes(cb_l, C, "cb_raw", "cb_raw")
-        cb_scales = deal_bytes(cb_raw, "cb_scales")
-        xq_words = sb.tile([P, S], U32, name="xq_words", align_bytes=64)
-        nc.vector.tensor_copy(xq_words[:], x_sb[:].indirect(offs_l[:]))
 
         def product(out, words, scales, t, rhs_words, rhs_scales):
             cols = slice(t * P, (t + 1) * P)
@@ -120,107 +117,136 @@ def tile_picked_ccmppathbhopb_none_po_kernel(
                 stop=True,
             )
 
+        def fetch(out, win, offsets, scale=1.0):
+            nc.scalar.activation(out, win.indirect(offsets), COPY, scale=scale)
+
+        def four_by_four(planes):
+            return planes.rearrange("p t (c i) -> p c t i", i=4)
+
+        def packed(words):
+            return words.rearrange("p (c i) t -> p c t i", i=4)
+
+        def quantise(words, scales, src):
+            nc.vector.quantize_mx(
+                out=words[:].bitcast(FP8X4), scales=scales[:], in_=src[:].rearrange("p j t -> p (j t)")
+            )
+
+        w_dealt = sb.tile([P, H], U32, name="w_dealt", align_bytes=64)
+        nc.vector.tensor_copy(
+            w_dealt[:].rearrange("p (t c i) -> p c t i", t=PACK, i=4),
+            w_words[:].rearrange("p (c i t) -> p c t i", t=PACK, i=4),
+        )
+        xq_scales = gather_bytes(offs_l, S, "xq_scales", "picked_bytes")
+        ca_raw = gather_bytes(ca_l, C, "ca_raw", "ca_raw")
+        xq_words = sb.tile([P, S], U32, name="xq_words", align_bytes=64)
+        nc.vector.tensor_copy(xq_words[:], x_sb[:].indirect(offs_l[:]))
+        w_scales = deal_bytes(w_plane, "w_scales", "w_scales")
+
         y_ps = [ps.tile([P, S], F32, name="y_ps%d" % t, tag="bank%d" % t) for t in range(PACK)]
         for t in range(PACK):
             product(y_ps[t][:], w_dealt, w_scales, t, xq_words[:], xq_scales[:])
 
-        ca_words = gather_words_dealt(ca_l, "ca_words")
-        cb_words = gather_words_dealt(cb_l, "cb_words")
+        ca_words = shared.tile([P, C], U32, name="ca_words", offset=0, align_bytes=64)
+        nc.vector.tensor_copy(ca_words[:].rearrange("p (t m) -> p m t", t=PACK), x_sb[:].indirect(ca_l[:]))
+        ca_scales = deal_bytes(ca_raw, "ca_scales", "ca_scales")
+        cb_raw = shared.tile([P, C], U8, name="cb_raw", offset=4 * C, align_bytes=64)
+        nc.vector.tensor_copy(cb_raw[:], x_plane[:].indirect(cb_l[:]))
+        cb_scales = deal_bytes(cb_raw, "cb_scales", "cb_scales")
 
-        y_n1 = [sb.tile([P, S], F32, name="y_n1_%d" % t) for t in range(PACK)]
-        st = [sb.tile([P, S], F32, name="st%d" % t) for t in range(PACK)]
-        own = [sb.tile([P, S], F32, name="own%d" % t) for t in range(PACK)]
+        y_n1 = [sb.tile([P, S], F32, name="y_n1_%d" % t, tag="y_n1_%d" % t, align_bytes=64) for t in range(PACK)]
+        nc.scalar.activation(y_neg[:, plane(0)], y_ps[0][:], COPY, scale=-0.5)
         for t in range(PACK):
-            nc.scalar.activation(y_sb[t][:, :S], y_ps[t][:], COPY)
-            nc.scalar.activation(y_n1[t][:], y_sb[t][:].indirect(n1_l[:]), COPY)
-        for t in range(PACK):
-            nc.vector.tensor_tensor(st[t][:], y_n1[t][:], y_sb[t][:, :S], ALU.max)
-            nc.vector.tensor_scalar(own[t][:], y_sb[t][:, :S], neg_half_gs[:, t : t + 1], None, ALU.mult)
+            if t + 1 < PACK:
+                nc.scalar.activation(y_neg[:, plane(t + 1)], y_ps[t + 1][:], COPY, scale=-0.5)
+            fetch(y_n1[t][:], y_neg[:, plane(t, 2)], n1_l[:], scale=-2.0)
 
-        st_n2 = sb.tile([P, PACK, S], F32, name="st_n2")
+        st_n2 = sb.tile([P, 2, S], F32, name="st_n2")
+        own = sb.tile([P, 2, S], F32, name="own")
+        diff = sb.tile([P, 2, S], F32, name="diff")
         z_f32 = sb.tile([P, PACK, S], F32, name="z_f32")
         z_bf = sb.tile([P, S, PACK], BF16, name="z_bf", align_bytes=64)
         z_words = sb.tile([P, S], U32, name="z_words", align_bytes=64)
         z_scales = sb.tile([P, S], U8, name="z_scales", align_bytes=64)
 
-        def interleave(engine_copy, dst, src, h):
-            engine_copy(
-                dst[:, half_cols(h), :].rearrange("p (c i) t -> p c t i", i=4),
-                src[:, :, half_cols(h)].rearrange("p t (c i) -> p c t i", i=4),
-            )
+        def make_st(t):
+            nc.vector.scalar_tensor_tensor(st[t][:, :S], y_neg[:, plane(t)], -2.0, y_n1[t][:], ALU.mult, ALU.max)
 
-        def quantise(words, scales, src, h):
-            nc.vector.quantize_mx(
-                out=words[:, half_cols(h)].bitcast(FP8X4),
-                scales=scales[:, half_cols(h)],
-                in_=src[:, half_cols(h), :].rearrange("p j t -> p (j t)"),
-            )
+        def weight(t):
+            return gs_sb[:, t : t + 1]
 
-        a_sb = [sb.tile([P, S], F32, name="a_sb%d" % t) for t in range(PACK)]
-        b_sb = [sb.tile([P, S], F32, name="b_sb%d" % t) for t in range(PACK)]
+        make_st(0)
+        make_st(1)
+        cb_words = gather_words_dealt(cb_l, "cb_words", "y_n1_1")
+        make_st(2)
+        make_st(3)
+        for t in range(2):
+            fetch(st_n2[:, t, :], st[t][:], n2_l[:])
+            nc.scalar.activation(own[:, t, :], y_neg[:, plane(t)], COPY, scale=weight(t))
+        for t in range(2, PACK):
+            nc.vector.tensor_tensor(diff[:, t - 2, :], st[t][:].indirect(n2_l[:]), y_neg[:, plane(t)], ALU.add)
+            nc.scalar.activation(z_f32[:, t, :], diff[:, t - 2, :], COPY, scale=weight(t))
+        for t in range(2):
+            nc.vector.scalar_tensor_tensor(z_f32[:, t, :], st_n2[:, t, :], weight(t), own[:, t, :], ALU.mult, ALU.add)
+        nc.vector.tensor_copy(packed(z_bf[:]), four_by_four(z_f32[:]))
+        quantise(z_words, z_scales, z_bf)
 
-        for h in range(2):
-            for t in range(PACK):
-                nc.scalar.activation(st_n2[:, t, half_cols(h)], st[t][:].indirect(half_list(n2_l, h)), COPY)
-                nc.vector.scalar_tensor_tensor(
-                    z_f32[:, t, half_cols(h)],
-                    st_n2[:, t, half_cols(h)],
-                    gs_sb[:, t : t + 1],
-                    own[t][:, half_cols(h)],
-                    ALU.mult,
-                    ALU.add,
-                )
-            interleave(nc.vector.tensor_copy, z_bf, z_f32, h)
-            quantise(z_words, z_scales, z_bf, h)
-
-        first_a = ps.tile([P, PACK, HALF], F32, name="first_a")
-        first_b = ps.tile([P, PACK, HALF], F32, name="first_b")
+        a_ps = [ps.tile([P, S], F32, name="a_ps%d" % t, tag="bank%d" % t) for t in range(PACK)]
+        b_ps = [ps.tile([P, S], F32, name="b_ps%d" % t, tag="bank%d" % (PACK + t)) for t in range(PACK)]
+        last = PACK - 1
+        product(a_ps[0][:], ca_words, ca_scales, 0, z_words[:], z_scales[:])
         for t in range(PACK):
-            product(first_a[:, t, :], ca_words, ca_scales, t, z_words[:, half_cols(0)], z_scales[:, half_cols(0)])
-        for t in range(PACK):
-            product(first_b[:, t, :], cb_words, cb_scales, t, z_words[:, half_cols(0)], z_scales[:, half_cols(0)])
-        for t in range(PACK):
-            nc.scalar.activation(a_sb[t][:, half_cols(0)], first_a[:, t, :], COPY, scale=0.0625)
-        for t in range(PACK):
-            nc.scalar.activation(b_sb[t][:, half_cols(0)], first_b[:, t, :], COPY, scale=0.0625)
+            product(b_ps[t][:], cb_words, cb_scales, t, z_words[:], z_scales[:])
+        for t in range(1, PACK):
+            product(a_ps[t][:], ca_words, ca_scales, t, z_words[:], z_scales[:])
 
-        a_n3 = sb.tile([P, PACK, S], F32, name="a_n3")
-        a_n4 = sb.tile([P, PACK, S], F32, name="a_n4")
-        sum35 = sb.tile([P, PACK, S], F32, name="sum35")
-        sum46 = sb.tile([P, PACK, S], F32, name="sum46")
+        a_got = sb.tile([P, PACK, 2, S], F32, name="a_got")
+        sums = sb.tile([P, PACK, 2, S], F32, name="sums")
         o_f32 = sb.tile([P, PACK, S], F32, name="o_f32")
         o_bf = sb.tile([P, S, PACK], BF16, name="o_bf", align_bytes=64)
         o_words = sb.tile([P, S], U32, name="o_words", align_bytes=64)
         o_scales = sb.tile([P, S], U8, name="o_scales", align_bytes=64)
         out_rows = out_0.rearrange("(p t) j -> p t j", t=PACK)
         out_words = out_1[0].rearrange("p n t -> p (n t)").bitcast(I32)
+        a_lists = (n3_l, n4_l)
+        b_lists = (n5_l, n6_l)
+        b_got = sb.tile([P, S], F32, name="b_got")
 
-        for h in range(2):
-            cols = half_cols(h)
-            for t in range(PACK):
-                if h == 0:
-                    second_a = ps.tile([P, HALF], F32, name="second_a", tag="bank%d" % t)
-                    second_b = ps.tile([P, HALF], F32, name="second_b", tag="late_b%d" % (t % 2))
-                    product(second_a[:], ca_words, ca_scales, t, z_words[:, half_cols(1)], z_scales[:, half_cols(1)])
-                    product(second_b[:], cb_words, cb_scales, t, z_words[:, half_cols(1)], z_scales[:, half_cols(1)])
-                    nc.scalar.activation(a_sb[t][:, half_cols(1)], second_a[:], COPY, scale=0.0625)
-                    if t < 2:
-                        nc.vector.tensor_scalar(b_sb[t][:, half_cols(1)], second_b[:], 0.0625, None, ALU.mult)
-                    else:
-                        nc.scalar.activation(b_sb[t][:, half_cols(1)], second_b[:], COPY, scale=0.0625)
-                nc.scalar.activation(a_n3[:, t, cols], a_sb[t][:].indirect(half_list(n3_l, h)), COPY)
-                nc.scalar.activation(a_n4[:, t, cols], a_sb[t][:].indirect(half_list(n4_l, h)), COPY)
-                nc.vector.tensor_tensor(
-                    sum35[:, t, cols], b_sb[t][:].indirect(half_list(n5_l, h)), a_n3[:, t, cols], ALU.add
-                )
-                nc.vector.tensor_tensor(
-                    sum46[:, t, cols], b_sb[t][:].indirect(half_list(n6_l, h)), a_n4[:, t, cols], ALU.add
-                )
-                nc.vector.tensor_tensor(o_f32[:, t, cols], sum35[:, t, cols], sum46[:, t, cols], ALU.max)
-            nc.sync.dma_start(out_rows[:, :, cols], o_f32[:, :, cols])
-            interleave(nc.vector.tensor_copy, o_bf, o_f32, h)
-            quantise(o_words, o_scales, o_bf, h)
-            nc.sync.dma_start(out_words[:, cols], o_words[:, cols].bitcast(I32))
+        def leave_a(t):
+            nc.scalar.activation(a_sb[t][:, :S], a_ps[t][:], COPY, scale=0.0625)
+
+        for t in range(PACK):
+            nc.vector.tensor_scalar(b_sb[t][:, :S], b_ps[t][:], 0.0625, None, ALU.mult)
+        leave_a(0)
+        for t in range(PACK):
+            if t == 1:
+                leave_a(1)
+            if 0 < t < last:
+                leave_a(t + 1)
+            for s in range(2):
+                fetch(a_got[:, t, s, :], a_sb[t][:], a_lists[s][:])
+        fetch(b_got[:], b_sb[last][:], b_lists[1][:])
+
+        def fetch_and_add(t, s):
+            nc.vector.tensor_tensor(sums[:, t, s, :], b_sb[t][:].indirect(b_lists[s][:]), a_got[:, t, s, :], ALU.add)
+
+        def finish(planes):
+            nc.vector.tensor_tensor(o_f32[:, planes, :], sums[:, planes, 0, :], sums[:, planes, 1, :], ALU.max)
+            nc.sync.dma_start(out_rows[:, planes, :], o_f32[:, planes, :])
+
+        for t in range(PACK):
+            fetch_and_add(t, 0)
+            if t == 2:
+                finish(slice(0, 2))
+            if t == last:
+                finish(slice(2, 3))
+            if t < last:
+                fetch_and_add(t, 1)
+        nc.vector.tensor_tensor(sums[:, last, 1, :], b_got[:], a_got[:, last, 1, :], ALU.add)
+        finish(slice(last, PACK))
+        nc.vector.tensor_copy(packed(o_bf[:, :ON_VECTOR, :]), four_by_four(o_f32[:, :, :ON_VECTOR]))
+        nc.scalar.activation(packed(o_bf[:, ON_VECTOR:, :]), four_by_four(o_f32[:, :, ON_VECTOR:]), COPY)
+        quantise(o_words, o_scales, o_bf)
+        nc.sync.dma_start(out_words, o_words[:].bitcast(I32))
         for q in range(4):
             queue = nc.scalar if q % 2 == 0 else nc.sync
             queue.dma_start(out_2[0, 4 * q : 4 * q + 4, :].bitcast(I32), o_scales[32 * q : 32 * q + 4, :].bitcast(I32))

@@ -20,7 +20,7 @@ PACK = 4
 HALF = S // 2
 SPARE = 16
 PER_COL = 16
-ON_VECTOR = 176
+ON_VECTOR = 192
 
 
 def tile_picked_ccmppathbhopb_none_po_kernel(
@@ -37,13 +37,11 @@ def tile_picked_ccmppathbhopb_none_po_kernel(
             nc.sync.dma_start(lst[:], src)
             return lst
 
-        def load_words(queue, src, cols, name):
-            words = sb.tile([P, cols], U32, name=name, align_bytes=64)
-            queue.dma_start(words[:].bitcast(I32), src[0].rearrange("p n t -> p (n t)").bitcast(I32))
-            return words
+        def load_words(words, src):
+            nc.sync.dma_start(words[:].bitcast(I32), src[0].rearrange("p n t -> p (n t)").bitcast(I32))
 
-        def load_scale_rows(plane, src):
-            for q in range(4):
+        def load_scale_rows(plane, src, quadrants):
+            for q in quadrants:
                 nc.sync.dma_start(plane[32 * q : 32 * q + 4, :].bitcast(I32), src[0, 4 * q : 4 * q + 4, :].bitcast(I32))
 
         def half_cols(h):
@@ -56,14 +54,13 @@ def tile_picked_ccmppathbhopb_none_po_kernel(
             return slice(t * S, (t + planes) * S)
 
         x_plane = sb.tile([P, T], U8, name="x_plane", align_bytes=64)
-        nc.vector.memset(x_plane[:, : T // 2].bitcast(I32), 0)
-        nc.gpsimd.memset(x_plane[:, T // 2 :].bitcast(I32), 0)
-        w_plane = shared.tile([P, H], U8, name="w_plane", offset=4 * C - H // 2, align_bytes=64)
+        nc.vector.memset(x_plane[:].bitcast(I32), 0)
+        w_plane = sb.tile([P, H], U8, name="w_plane", align_bytes=64)
         nc.vector.memset(w_plane[:].bitcast(I32), 0)
 
         def window(name):
             win = sb.tile([P, S + SPARE], F32, name=name)
-            nc.gpsimd.memset(win[:, S:], 0.0)
+            nc.vector.memset(win[:, S:], 0.0)
             return win
 
         y_neg = sb.tile([P, (PACK + 1) * S], F32, name="y_neg")
@@ -73,13 +70,16 @@ def tile_picked_ccmppathbhopb_none_po_kernel(
         b_sb = [window("b_sb%d" % t) for t in range(PACK)]
 
         offs_l = load_list(offs, "offs_l")
-        w_words = load_words(nc.scalar, w1_words, H, "w_words")
-        load_scale_rows(x_plane, x_scales)
         ca_l = load_list(ca, "ca_l")
-        x_sb = load_words(nc.sync, x_words, T, "x_sb")
-        load_scale_rows(w_plane, w1_scales)
-        n1_l = load_list(n1, "n1_l")
         cb_l = load_list(cb, "cb_l")
+        load_scale_rows(x_plane, x_scales, range(4))
+        load_scale_rows(w_plane, w1_scales, range(1))
+        x_sb = sb.tile([P, T], U32, name="x_sb", align_bytes=64)
+        load_words(x_sb, x_words)
+        load_scale_rows(w_plane, w1_scales, range(1, 4))
+        w_words = shared.tile([P, H], U32, name="w_words", offset=1024, align_bytes=64)
+        load_words(w_words, w1_words)
+        n1_l = load_list(n1, "n1_l")
         n2_l = load_list(n2, "n2_l")
         gs_sb = sb.tile([P, PACK], F32, name="gs_sb")
         nc.sync.dma_start(gs_sb[:], gs.rearrange("(p t) o -> p (t o)", t=PACK))
@@ -88,22 +88,18 @@ def tile_picked_ccmppathbhopb_none_po_kernel(
         n4_l = load_list(n4, "n4_l")
         n6_l = load_list(n6, "n6_l")
 
-        def deal_bytes(raw, name, tag):
-            dealt = sb.tile([P, C], U8, name=name, tag=tag, align_bytes=64)
+        def deal_bytes(dealt, raw):
             nc.vector.tensor_copy(
                 dealt[:].rearrange("p (t m) -> p t m", t=PACK), raw[:].rearrange("p (m t) -> p t m", t=PACK)
             )
-            return dealt
 
-        def gather_bytes(lst, cols, name, tag):
-            got = sb.tile([P, cols], U8, name=name, tag=tag, align_bytes=64)
+        def gather_bytes(lst, cols, name):
+            got = sb.tile([P, cols], U8, name=name, align_bytes=64)
             nc.vector.tensor_copy(got[:], x_plane[:].indirect(lst[:]))
             return got
 
-        def gather_words_dealt(lst, name, tag):
-            got = sb.tile([P, C], U32, name=name, tag=tag, align_bytes=64)
+        def gather_words_dealt(got, lst):
             nc.vector.tensor_copy(got[:].rearrange("p (t m) -> p m t", t=PACK), x_sb[:].indirect(lst[:]))
-            return got
 
         def product(out, words, scales, t, rhs_words, rhs_scales):
             cols = slice(t * P, (t + 1) * P)
@@ -126,68 +122,75 @@ def tile_picked_ccmppathbhopb_none_po_kernel(
         def packed(words):
             return words.rearrange("p (c i) t -> p c t i", i=4)
 
+        def round_and_pack(dst, src):
+            nc.vector.tensor_copy(packed(dst[:, :ON_VECTOR, :]), four_by_four(src[:, :, :ON_VECTOR]))
+            nc.scalar.activation(packed(dst[:, ON_VECTOR:, :]), four_by_four(src[:, :, ON_VECTOR:]), COPY)
+
         def quantise(words, scales, src):
             nc.vector.quantize_mx(
                 out=words[:].bitcast(FP8X4), scales=scales[:], in_=src[:].rearrange("p j t -> p (j t)")
             )
 
-        w_dealt = sb.tile([P, H], U32, name="w_dealt", align_bytes=64)
+        xq_scales = gather_bytes(offs_l, S, "xq_scales")
+        ca_raw = gather_bytes(ca_l, C, "ca_raw")
+        cb_raw = gather_bytes(cb_l, C, "cb_raw")
+        xq_words = sb.tile([P, S], U32, name="xq_words", align_bytes=64)
+        nc.vector.tensor_copy(xq_words[:], x_sb[:].indirect(offs_l[:]))
+        w_scales = sb.tile([P, H], U8, name="w_scales", align_bytes=64)
+        deal_bytes(w_scales, w_plane)
+        w_dealt = sb.tile([P, C], U32, name="w_dealt", align_bytes=64)
         nc.vector.tensor_copy(
             w_dealt[:].rearrange("p (t c i) -> p c t i", t=PACK, i=4),
             w_words[:].rearrange("p (c i t) -> p c t i", t=PACK, i=4),
         )
-        xq_scales = gather_bytes(offs_l, S, "xq_scales", "picked_bytes")
-        ca_raw = gather_bytes(ca_l, C, "ca_raw", "ca_raw")
-        xq_words = sb.tile([P, S], U32, name="xq_words", align_bytes=64)
-        nc.vector.tensor_copy(xq_words[:], x_sb[:].indirect(offs_l[:]))
-        w_scales = deal_bytes(w_plane, "w_scales", "w_scales")
 
         y_ps = [ps.tile([P, S], F32, name="y_ps%d" % t, tag="bank%d" % t) for t in range(PACK)]
         for t in range(PACK):
             product(y_ps[t][:], w_dealt, w_scales, t, xq_words[:], xq_scales[:])
 
         ca_words = shared.tile([P, C], U32, name="ca_words", offset=0, align_bytes=64)
-        nc.vector.tensor_copy(ca_words[:].rearrange("p (t m) -> p m t", t=PACK), x_sb[:].indirect(ca_l[:]))
-        ca_scales = deal_bytes(ca_raw, "ca_scales", "ca_scales")
-        cb_raw = shared.tile([P, C], U8, name="cb_raw", offset=4 * C, align_bytes=64)
-        nc.vector.tensor_copy(cb_raw[:], x_plane[:].indirect(cb_l[:]))
-        cb_scales = deal_bytes(cb_raw, "cb_scales", "cb_scales")
+        cb_words = shared.tile([P, C], U32, name="cb_words", offset=2048, align_bytes=64)
+        gather_words_dealt(ca_words, ca_l)
+        gather_words_dealt(cb_words, cb_l)
 
-        y_n1 = [sb.tile([P, S], F32, name="y_n1_%d" % t, tag="y_n1_%d" % t, align_bytes=64) for t in range(PACK)]
+        y_n1 = sb.tile([P, PACK, S], F32, name="y_n1")
         nc.scalar.activation(y_neg[:, plane(0)], y_ps[0][:], COPY, scale=-0.5)
         for t in range(PACK):
             if t + 1 < PACK:
                 nc.scalar.activation(y_neg[:, plane(t + 1)], y_ps[t + 1][:], COPY, scale=-0.5)
-            fetch(y_n1[t][:], y_neg[:, plane(t, 2)], n1_l[:], scale=-2.0)
+            fetch(y_n1[:, t, :], y_neg[:, plane(t, 2)], n1_l[:], scale=-2.0)
 
-        st_n2 = sb.tile([P, 2, S], F32, name="st_n2")
-        own = sb.tile([P, 2, S], F32, name="own")
-        diff = sb.tile([P, 2, S], F32, name="diff")
+        st_n2 = {t: sb.tile([P, S], F32, name="st_n2_%d" % t, tag="st_n2_%d" % t, align_bytes=64) for t in range(1, PACK)}
+        own = sb.tile([P, PACK - 1, S], F32, name="own")
+        diff = sb.tile([P, S], F32, name="diff")
         z_f32 = sb.tile([P, PACK, S], F32, name="z_f32")
         z_bf = sb.tile([P, S, PACK], BF16, name="z_bf", align_bytes=64)
         z_words = sb.tile([P, S], U32, name="z_words", align_bytes=64)
         z_scales = sb.tile([P, S], U8, name="z_scales", align_bytes=64)
 
         def make_st(t):
-            nc.vector.scalar_tensor_tensor(st[t][:, :S], y_neg[:, plane(t)], -2.0, y_n1[t][:], ALU.mult, ALU.max)
+            nc.vector.scalar_tensor_tensor(st[t][:, :S], y_neg[:, plane(t)], -2.0, y_n1[:, t, :], ALU.mult, ALU.max)
 
         def weight(t):
             return gs_sb[:, t : t + 1]
 
         make_st(0)
-        make_st(1)
-        cb_words = gather_words_dealt(cb_l, "cb_words", "y_n1_1")
-        make_st(2)
-        make_st(3)
-        for t in range(2):
-            fetch(st_n2[:, t, :], st[t][:], n2_l[:])
-            nc.scalar.activation(own[:, t, :], y_neg[:, plane(t)], COPY, scale=weight(t))
-        for t in range(2, PACK):
-            nc.vector.tensor_tensor(diff[:, t - 2, :], st[t][:].indirect(n2_l[:]), y_neg[:, plane(t)], ALU.add)
-            nc.scalar.activation(z_f32[:, t, :], diff[:, t - 2, :], COPY, scale=weight(t))
-        for t in range(2):
-            nc.vector.scalar_tensor_tensor(z_f32[:, t, :], st_n2[:, t, :], weight(t), own[:, t, :], ALU.mult, ALU.add)
-        nc.vector.tensor_copy(packed(z_bf[:]), four_by_four(z_f32[:]))
+        nc.vector.tensor_tensor(diff[:], st[0][:].indirect(n2_l[:]), y_neg[:, plane(0)], ALU.add)
+        for t in range(1, PACK):
+            make_st(t)
+        for t in range(1, PACK):
+            nc.vector.tensor_scalar(own[:, t - 1, :], y_neg[:, plane(t)], weight(t), None, ALU.mult)
+        nc.vector.tensor_scalar(z_f32[:, 0, :], diff[:], weight(0), None, ALU.mult)
+        for t in range(1, PACK):
+            fetch(st_n2[t][:], st[t][:], n2_l[:])
+            nc.vector.scalar_tensor_tensor(
+                z_f32[:, t, :], st_n2[t][:], weight(t), own[:, t - 1, :], ALU.mult, ALU.add
+            )
+        ca_scales = sb.tile([P, C], U8, name="ca_scales", tag="st_n2_2", align_bytes=64)
+        deal_bytes(ca_scales, ca_raw)
+        round_and_pack(z_bf, z_f32)
+        cb_scales = sb.tile([P, C], U8, name="cb_scales", tag="st_n2_3", align_bytes=64)
+        deal_bytes(cb_scales, cb_raw)
         quantise(z_words, z_scales, z_bf)
 
         a_ps = [ps.tile([P, S], F32, name="a_ps%d" % t, tag="bank%d" % t) for t in range(PACK)]
@@ -209,7 +212,7 @@ def tile_picked_ccmppathbhopb_none_po_kernel(
         out_words = out_1[0].rearrange("p n t -> p (n t)").bitcast(I32)
         a_lists = (n3_l, n4_l)
         b_lists = (n5_l, n6_l)
-        b_got = sb.tile([P, S], F32, name="b_got")
+        b_got = sb.tile([P, 2, S], F32, name="b_got")
 
         def leave_a(t):
             nc.scalar.activation(a_sb[t][:, :S], a_ps[t][:], COPY, scale=0.0625)
@@ -224,7 +227,8 @@ def tile_picked_ccmppathbhopb_none_po_kernel(
                 leave_a(t + 1)
             for s in range(2):
                 fetch(a_got[:, t, s, :], a_sb[t][:], a_lists[s][:])
-        fetch(b_got[:], b_sb[last][:], b_lists[1][:])
+                if t == last:
+                    fetch(b_got[:, s, :], b_sb[last][:], b_lists[s][:])
 
         def fetch_and_add(t, s):
             nc.vector.tensor_tensor(sums[:, t, s, :], b_sb[t][:].indirect(b_lists[s][:]), a_got[:, t, s, :], ALU.add)
@@ -233,18 +237,19 @@ def tile_picked_ccmppathbhopb_none_po_kernel(
             nc.vector.tensor_tensor(o_f32[:, planes, :], sums[:, planes, 0, :], sums[:, planes, 1, :], ALU.max)
             nc.sync.dma_start(out_rows[:, planes, :], o_f32[:, planes, :])
 
-        for t in range(PACK):
+        def add_last(s):
+            nc.vector.tensor_tensor(sums[:, last, s, :], b_got[:, s, :], a_got[:, last, s, :], ALU.add)
+
+        for t in range(last):
             fetch_and_add(t, 0)
             if t == 2:
                 finish(slice(0, 2))
-            if t == last:
-                finish(slice(2, 3))
-            if t < last:
-                fetch_and_add(t, 1)
-        nc.vector.tensor_tensor(sums[:, last, 1, :], b_got[:], a_got[:, last, 1, :], ALU.add)
+            fetch_and_add(t, 1)
+        add_last(0)
+        finish(slice(2, 3))
+        add_last(1)
         finish(slice(last, PACK))
-        nc.vector.tensor_copy(packed(o_bf[:, :ON_VECTOR, :]), four_by_four(o_f32[:, :, :ON_VECTOR]))
-        nc.scalar.activation(packed(o_bf[:, ON_VECTOR:, :]), four_by_four(o_f32[:, :, ON_VECTOR:]), COPY)
+        round_and_pack(o_bf, o_f32)
         quantise(o_words, o_scales, o_bf)
         nc.sync.dma_start(out_words, o_words[:].bitcast(I32))
         for q in range(4):

@@ -17,9 +17,14 @@ COPY = mybir.ActivationFunctionType.Copy
 
 P = 128
 PACK = 4
+LAST = PACK - 1
 HALF = S // 2
 SPARE = 16
 PER_COL = 16
+QUADRANTS = 4
+LINE = 4
+WORD_BYTES = 4
+SIXTEENTH = 0.0625
 ON_VECTOR = 192
 
 
@@ -32,18 +37,6 @@ def tile_picked_ccmppathbhopb_none_po_kernel(
         shared = ctx.enter_context(tc.tile_pool(name="shared", bufs=1))
         ps = ctx.enter_context(tc.psum_pool(name="ps", bufs=1))
 
-        def load_list(src, name):
-            lst = sb.tile(list(src.shape), U16, name=name)
-            nc.sync.dma_start(lst[:], src)
-            return lst
-
-        def load_words(words, src):
-            nc.sync.dma_start(words[:].bitcast(I32), src[0].rearrange("p n t -> p (n t)").bitcast(I32))
-
-        def load_scale_rows(plane, src, quadrants):
-            for q in quadrants:
-                nc.sync.dma_start(plane[32 * q : 32 * q + 4, :].bitcast(I32), src[0, 4 * q : 4 * q + 4, :].bitcast(I32))
-
         def half_cols(h):
             return slice(h * HALF, (h + 1) * HALF)
 
@@ -53,31 +46,49 @@ def tile_picked_ccmppathbhopb_none_po_kernel(
         def plane(t, planes=1):
             return slice(t * S, (t + planes) * S)
 
-        x_plane = sb.tile([P, T], U8, name="x_plane", align_bytes=64)
-        nc.vector.memset(x_plane[:].bitcast(I32), 0)
-        w_plane = sb.tile([P, H], U8, name="w_plane", align_bytes=64)
-        nc.vector.memset(w_plane[:].bitcast(I32), 0)
+        x_bytes = sb.tile([P, T], U8, name="x_bytes", align_bytes=64)
+        nc.vector.memset(x_bytes[:].bitcast(I32), 0)
+        w_bytes = sb.tile([P, H], U8, name="w_bytes", align_bytes=64)
+        nc.vector.memset(w_bytes[:].bitcast(I32), 0)
 
-        def window(name):
+        def one_plane_window(name):
             win = sb.tile([P, S + SPARE], F32, name=name)
             nc.vector.memset(win[:, S:], 0.0)
             return win
 
-        y_neg = sb.tile([P, (PACK + 1) * S], F32, name="y_neg")
-        nc.vector.memset(y_neg[:, plane(PACK)], 0.0)
-        st = [window("st%d" % t) for t in range(PACK)]
-        a_sb = [window("a_sb%d" % t) for t in range(PACK)]
-        b_sb = [window("b_sb%d" % t) for t in range(PACK)]
+        def four_plane_window(name):
+            win = sb.tile([P, (PACK + 1) * S], F32, name=name)
+            nc.vector.memset(win[:, plane(PACK)], 0.0)
+            return win
+
+        y_neg = four_plane_window("y_neg")
+        st = [one_plane_window("st0")] + [sb.tile([P, S], F32, name="st%d" % t) for t in range(1, PACK)]
+        a_sb = four_plane_window("a_sb")
+        b_sb = [one_plane_window("b_sb%d" % t) for t in range(PACK)]
+
+        def load_list(src, name):
+            lst = sb.tile(list(src.shape), U16, name=name)
+            nc.sync.dma_start(lst[:], src)
+            return lst
+
+        def load_words(words, src):
+            nc.sync.dma_start(words[:].bitcast(I32), src[0].rearrange("p n t -> p (n t)").bitcast(I32))
+
+        def load_scale_rows(scale_tile, src, quadrants):
+            for q in quadrants:
+                nc.sync.dma_start(
+                    scale_tile[32 * q : 32 * q + 4, :].bitcast(I32), src[0, 4 * q : 4 * q + 4, :].bitcast(I32)
+                )
 
         offs_l = load_list(offs, "offs_l")
         ca_l = load_list(ca, "ca_l")
         cb_l = load_list(cb, "cb_l")
-        load_scale_rows(x_plane, x_scales, range(4))
-        load_scale_rows(w_plane, w1_scales, range(1))
+        load_scale_rows(x_bytes, x_scales, range(QUADRANTS))
+        load_scale_rows(w_bytes, w1_scales, range(1))
         x_sb = sb.tile([P, T], U32, name="x_sb", align_bytes=64)
         load_words(x_sb, x_words)
-        load_scale_rows(w_plane, w1_scales, range(1, 4))
-        w_words = shared.tile([P, H], U32, name="w_words", offset=1024, align_bytes=64)
+        load_scale_rows(w_bytes, w1_scales, range(1, QUADRANTS))
+        w_words = shared.tile([P, H], U32, name="w_words", offset=C * WORD_BYTES // 2, align_bytes=64)
         load_words(w_words, w1_words)
         n1_l = load_list(n1, "n1_l")
         n2_l = load_list(n2, "n2_l")
@@ -88,15 +99,15 @@ def tile_picked_ccmppathbhopb_none_po_kernel(
         n4_l = load_list(n4, "n4_l")
         n6_l = load_list(n6, "n6_l")
 
+        def gather_bytes(lst, cols, name):
+            got = sb.tile([P, cols], U8, name=name, align_bytes=64)
+            nc.vector.tensor_copy(got[:], x_bytes[:].indirect(lst[:]))
+            return got
+
         def deal_bytes(dealt, raw):
             nc.vector.tensor_copy(
                 dealt[:].rearrange("p (t m) -> p t m", t=PACK), raw[:].rearrange("p (m t) -> p t m", t=PACK)
             )
-
-        def gather_bytes(lst, cols, name):
-            got = sb.tile([P, cols], U8, name=name, align_bytes=64)
-            nc.vector.tensor_copy(got[:], x_plane[:].indirect(lst[:]))
-            return got
 
         def gather_words_dealt(got, lst):
             nc.vector.tensor_copy(got[:].rearrange("p (t m) -> p m t", t=PACK), x_sb[:].indirect(lst[:]))
@@ -116,20 +127,14 @@ def tile_picked_ccmppathbhopb_none_po_kernel(
         def fetch(out, win, offsets, scale=1.0):
             nc.scalar.activation(out, win.indirect(offsets), COPY, scale=scale)
 
-        def four_by_four(planes):
-            return planes.rearrange("p t (c i) -> p c t i", i=4)
+        def as_planes(planes):
+            return planes.rearrange("p t (c i) -> p c t i", i=LINE)
 
-        def packed(words):
-            return words.rearrange("p (c i) t -> p c t i", i=4)
+        def as_words(rounded):
+            return rounded.rearrange("p (c i) t -> p c t i", i=LINE)
 
-        def round_and_pack(dst, src):
-            nc.vector.tensor_copy(packed(dst[:, :ON_VECTOR, :]), four_by_four(src[:, :, :ON_VECTOR]))
-            nc.scalar.activation(packed(dst[:, ON_VECTOR:, :]), four_by_four(src[:, :, ON_VECTOR:]), COPY)
-
-        def quantise(words, scales, src):
-            nc.vector.quantize_mx(
-                out=words[:].bitcast(FP8X4), scales=scales[:], in_=src[:].rearrange("p j t -> p (j t)")
-            )
+        def quantise(words, scales, rounded):
+            nc.vector.quantize_mx(out=words.bitcast(FP8X4), scales=scales, in_=rounded.rearrange("p j t -> p (j t)"))
 
         xq_scales = gather_bytes(offs_l, S, "xq_scales")
         ca_raw = gather_bytes(ca_l, C, "ca_raw")
@@ -137,11 +142,11 @@ def tile_picked_ccmppathbhopb_none_po_kernel(
         xq_words = sb.tile([P, S], U32, name="xq_words", align_bytes=64)
         nc.vector.tensor_copy(xq_words[:], x_sb[:].indirect(offs_l[:]))
         w_scales = sb.tile([P, H], U8, name="w_scales", align_bytes=64)
-        deal_bytes(w_scales, w_plane)
-        w_dealt = sb.tile([P, C], U32, name="w_dealt", align_bytes=64)
+        deal_bytes(w_scales, w_bytes)
+        w_dealt = sb.tile([P, H], U32, name="w_dealt", align_bytes=64)
         nc.vector.tensor_copy(
-            w_dealt[:].rearrange("p (t c i) -> p c t i", t=PACK, i=4),
-            w_words[:].rearrange("p (c i t) -> p c t i", t=PACK, i=4),
+            w_dealt[:].rearrange("p (t c i) -> p c t i", t=PACK, i=LINE),
+            w_words[:].rearrange("p (c i t) -> p c t i", t=PACK, i=LINE),
         )
 
         y_ps = [ps.tile([P, S], F32, name="y_ps%d" % t, tag="bank%d" % t) for t in range(PACK)]
@@ -149,19 +154,23 @@ def tile_picked_ccmppathbhopb_none_po_kernel(
             product(y_ps[t][:], w_dealt, w_scales, t, xq_words[:], xq_scales[:])
 
         ca_words = shared.tile([P, C], U32, name="ca_words", offset=0, align_bytes=64)
-        cb_words = shared.tile([P, C], U32, name="cb_words", offset=2048, align_bytes=64)
+        cb_words = shared.tile([P, C], U32, name="cb_words", offset=C * WORD_BYTES, align_bytes=64)
         gather_words_dealt(ca_words, ca_l)
         gather_words_dealt(cb_words, cb_l)
 
         y_n1 = sb.tile([P, PACK, S], F32, name="y_n1")
         nc.scalar.activation(y_neg[:, plane(0)], y_ps[0][:], COPY, scale=-0.5)
         for t in range(PACK):
-            if t + 1 < PACK:
+            if t < LAST:
                 nc.scalar.activation(y_neg[:, plane(t + 1)], y_ps[t + 1][:], COPY, scale=-0.5)
             fetch(y_n1[:, t, :], y_neg[:, plane(t, 2)], n1_l[:], scale=-2.0)
 
-        st_n2 = {t: sb.tile([P, S], F32, name="st_n2_%d" % t, tag="st_n2_%d" % t, align_bytes=64) for t in range(1, PACK)}
-        own = sb.tile([P, PACK - 1, S], F32, name="own")
+        st_n2 = {
+            (t, h): sb.tile([P, HALF], F32, name="st_n2_%d%d" % (t, h), tag="st_n2_%d%d" % (t, h), align_bytes=64)
+            for t in range(1, PACK)
+            for h in range(2)
+        }
+        own = sb.tile([P, LAST, S], F32, name="own")
         diff = sb.tile([P, S], F32, name="diff")
         z_f32 = sb.tile([P, PACK, S], F32, name="z_f32")
         z_bf = sb.tile([P, S, PACK], BF16, name="z_bf", align_bytes=64)
@@ -181,26 +190,42 @@ def tile_picked_ccmppathbhopb_none_po_kernel(
         for t in range(1, PACK):
             nc.vector.tensor_scalar(own[:, t - 1, :], y_neg[:, plane(t)], weight(t), None, ALU.mult)
         nc.vector.tensor_scalar(z_f32[:, 0, :], diff[:], weight(0), None, ALU.mult)
-        for t in range(1, PACK):
-            fetch(st_n2[t][:], st[t][:], n2_l[:])
-            nc.vector.scalar_tensor_tensor(
-                z_f32[:, t, :], st_n2[t][:], weight(t), own[:, t - 1, :], ALU.mult, ALU.add
-            )
-        ca_scales = sb.tile([P, C], U8, name="ca_scales", tag="st_n2_2", align_bytes=64)
-        deal_bytes(ca_scales, ca_raw)
-        round_and_pack(z_bf, z_f32)
-        cb_scales = sb.tile([P, C], U8, name="cb_scales", tag="st_n2_3", align_bytes=64)
-        deal_bytes(cb_scales, cb_raw)
-        quantise(z_words, z_scales, z_bf)
+        for h in range(2):
+            for t in range(1, PACK):
+                fetch(st_n2[t, h][:], st[t][:], half_list(n2_l, h))
 
-        a_ps = [ps.tile([P, S], F32, name="a_ps%d" % t, tag="bank%d" % t) for t in range(PACK)]
+        pair_scales = []
+        for h, (raw, name) in enumerate(((ca_raw, "ca_scales"), (cb_raw, "cb_scales"))):
+            cols = half_cols(h)
+            for t in range(1, PACK):
+                nc.vector.scalar_tensor_tensor(
+                    z_f32[:, t, cols], st_n2[t, h][:], weight(t), own[:, t - 1, cols], ALU.mult, ALU.add
+                )
+            nc.vector.tensor_copy(as_words(z_bf[:, cols, :]), as_planes(z_f32[:, :, cols]))
+            dealt = sb.tile([P, C], U8, name=name, tag="st_n2_%d%d" % (LAST, h), align_bytes=64)
+            deal_bytes(dealt, raw)
+            pair_scales.append(dealt)
+            quantise(z_words[:, cols], z_scales[:, cols], z_bf[:, cols, :])
+        ca_scales, cb_scales = pair_scales
+
+        def a_leaves_psum(planes, h, bank):
+            a_planes = a_sb[:, plane(0, PACK)].rearrange("p (t j) -> p t j", t=PACK)
+            nc.scalar.activation(a_planes[:, planes, half_cols(h)], bank, COPY, scale=SIXTEENTH)
+
+        z_half = [(z_words[:, half_cols(h)], z_scales[:, half_cols(h)]) for h in range(2)]
+        first_a = ps.tile([P, PACK, HALF], F32, name="first_a", tag="bank0")
+        for t in range(PACK):
+            product(first_a[:, t, :], ca_words, ca_scales, t, *z_half[0])
+        a_leaves_psum(slice(0, PACK), 0, first_a[:])
+
+        second_a = [ps.tile([P, 2, HALF], F32, name="second_a%d" % u, tag="bank%d" % (u + 1)) for u in range(2)]
         b_ps = [ps.tile([P, S], F32, name="b_ps%d" % t, tag="bank%d" % (PACK + t)) for t in range(PACK)]
-        last = PACK - 1
-        product(a_ps[0][:], ca_words, ca_scales, 0, z_words[:], z_scales[:])
+        for t in range(2):
+            product(second_a[0][:, t, :], ca_words, ca_scales, t, *z_half[1])
         for t in range(PACK):
             product(b_ps[t][:], cb_words, cb_scales, t, z_words[:], z_scales[:])
-        for t in range(1, PACK):
-            product(a_ps[t][:], ca_words, ca_scales, t, z_words[:], z_scales[:])
+        for t in range(2):
+            product(second_a[1][:, t, :], ca_words, ca_scales, 2 + t, *z_half[1])
 
         a_got = sb.tile([P, PACK, 2, S], F32, name="a_got")
         sums = sb.tile([P, PACK, 2, S], F32, name="sums")
@@ -208,50 +233,46 @@ def tile_picked_ccmppathbhopb_none_po_kernel(
         o_bf = sb.tile([P, S, PACK], BF16, name="o_bf", align_bytes=64)
         o_words = sb.tile([P, S], U32, name="o_words", align_bytes=64)
         o_scales = sb.tile([P, S], U8, name="o_scales", align_bytes=64)
+        b_got = sb.tile([P, 2, S], F32, name="b_got")
         out_rows = out_0.rearrange("(p t) j -> p t j", t=PACK)
-        out_words = out_1[0].rearrange("p n t -> p (n t)").bitcast(I32)
         a_lists = (n3_l, n4_l)
         b_lists = (n5_l, n6_l)
-        b_got = sb.tile([P, 2, S], F32, name="b_got")
-
-        def leave_a(t):
-            nc.scalar.activation(a_sb[t][:, :S], a_ps[t][:], COPY, scale=0.0625)
 
         for t in range(PACK):
-            nc.vector.tensor_scalar(b_sb[t][:, :S], b_ps[t][:], 0.0625, None, ALU.mult)
-        leave_a(0)
+            nc.vector.tensor_scalar(b_sb[t][:, :S], b_ps[t][:], SIXTEENTH, None, ALU.mult)
         for t in range(PACK):
-            if t == 1:
-                leave_a(1)
-            if 0 < t < last:
-                leave_a(t + 1)
+            if t < len(second_a):
+                a_leaves_psum(slice(2 * t, 2 * t + 2), 1, second_a[t][:])
             for s in range(2):
-                fetch(a_got[:, t, s, :], a_sb[t][:], a_lists[s][:])
-                if t == last:
-                    fetch(b_got[:, s, :], b_sb[last][:], b_lists[s][:])
+                fetch(a_got[:, t, s, :], a_sb[:, plane(t, 2)], a_lists[s][:])
+                if t == LAST:
+                    fetch(b_got[:, s, :], b_sb[LAST][:], b_lists[s][:])
 
         def fetch_and_add(t, s):
             nc.vector.tensor_tensor(sums[:, t, s, :], b_sb[t][:].indirect(b_lists[s][:]), a_got[:, t, s, :], ALU.add)
+
+        def add_last(s):
+            nc.vector.tensor_tensor(sums[:, LAST, s, :], b_got[:, s, :], a_got[:, LAST, s, :], ALU.add)
 
         def finish(planes):
             nc.vector.tensor_tensor(o_f32[:, planes, :], sums[:, planes, 0, :], sums[:, planes, 1, :], ALU.max)
             nc.sync.dma_start(out_rows[:, planes, :], o_f32[:, planes, :])
 
-        def add_last(s):
-            nc.vector.tensor_tensor(sums[:, last, s, :], b_got[:, s, :], a_got[:, last, s, :], ALU.add)
-
-        for t in range(last):
-            fetch_and_add(t, 0)
-            if t == 2:
-                finish(slice(0, 2))
-            fetch_and_add(t, 1)
+        for t in range(2):
+            for s in range(2):
+                fetch_and_add(t, s)
+        fetch_and_add(2, 0)
+        finish(slice(0, 2))
+        fetch_and_add(2, 1)
         add_last(0)
-        finish(slice(2, 3))
+        finish(slice(2, LAST))
         add_last(1)
-        finish(slice(last, PACK))
-        round_and_pack(o_bf, o_f32)
-        quantise(o_words, o_scales, o_bf)
-        nc.sync.dma_start(out_words, o_words[:].bitcast(I32))
-        for q in range(4):
+        finish(slice(LAST, PACK))
+
+        nc.vector.tensor_copy(as_words(o_bf[:, :ON_VECTOR, :]), as_planes(o_f32[:, :, :ON_VECTOR]))
+        nc.scalar.activation(as_words(o_bf[:, ON_VECTOR:, :]), as_planes(o_f32[:, :, ON_VECTOR:]), COPY)
+        quantise(o_words[:], o_scales[:], o_bf[:])
+        nc.sync.dma_start(out_1[0].rearrange("p n t -> p (n t)").bitcast(I32), o_words[:].bitcast(I32))
+        for q in range(QUADRANTS):
             queue = nc.scalar if q % 2 == 0 else nc.sync
             queue.dma_start(out_2[0, 4 * q : 4 * q + 4, :].bitcast(I32), o_scales[32 * q : 32 * q + 4, :].bitcast(I32))

from contextlib import ExitStack

import concourse.mybir as mybir

K, T, S, H, C = 512, 2048, 256, 512, 512
FLOPS = 2 * K * S * (H + 2 * C)

F32 = mybir.dt.float32
BF16 = mybir.dt.bfloat16
I32 = mybir.dt.int32
U32 = mybir.dt.uint32
U16 = mybir.dt.uint16
U8 = mybir.dt.uint8
FP8X4 = mybir.dt.float8_e4m3fn_x4
ALU = mybir.AluOpType
COPY = mybir.ActivationFunctionType.Copy

P = 128
PACK = 4
LAST = PACK - 1
HALF = S // 2
SPARE = 16
PER_COL = 16
QUADRANTS = 4
LINE = 4
WORD_BYTES = 4
SIXTEENTH = 0.0625
ON_VECTOR = 192


def tile_picked_ccmppathbhopb_none_po_kernel(
    tc, x_words, x_scales, w1_words, w1_scales, gs, offs, n1, n2, ca, cb, n3, n4, n5, n6, out_0, out_1, out_2
):
    nc = tc.nc
    with ExitStack() as ctx:
        sb = ctx.enter_context(tc.tile_pool(name="sb", bufs=1))
        shared = ctx.enter_context(tc.tile_pool(name="shared", bufs=1))
        ps = ctx.enter_context(tc.psum_pool(name="ps", bufs=1))

        def half_cols(h):
            return slice(h * HALF, (h + 1) * HALF)

        def half_list(lst, h):
            return lst[:, h * HALF // PER_COL : (h + 1) * HALF // PER_COL]

        def plane(t, planes=1):
            return slice(t * S, (t + planes) * S)

        x_bytes = sb.tile([P, T], U8, name="x_bytes", align_bytes=64)
        nc.vector.memset(x_bytes[:].bitcast(I32), 0)
        w_bytes = sb.tile([P, H], U8, name="w_bytes", align_bytes=64)
        nc.vector.memset(w_bytes[:].bitcast(I32), 0)

        def one_plane_window(name):
            win = sb.tile([P, S + SPARE], F32, name=name)
            nc.vector.memset(win[:, S:], 0.0)
            return win

        def four_plane_window(name):
            win = sb.tile([P, (PACK + 1) * S], F32, name=name)
            nc.vector.memset(win[:, plane(PACK)], 0.0)
            return win

        y_neg = four_plane_window("y_neg")
        st = [one_plane_window("st0")] + [sb.tile([P, S], F32, name="st%d" % t) for t in range(1, PACK)]
        a_sb = four_plane_window("a_sb")
        b_sb = [one_plane_window("b_sb%d" % t) for t in range(PACK)]

        def load_list(src, name):
            lst = sb.tile(list(src.shape), U16, name=name)
            nc.sync.dma_start(lst[:], src)
            return lst

        def load_words(words, src):
            nc.sync.dma_start(words[:].bitcast(I32), src[0].rearrange("p n t -> p (n t)").bitcast(I32))

        def load_scale_rows(scale_tile, src, quadrants):
            for q in quadrants:
                nc.sync.dma_start(
                    scale_tile[32 * q : 32 * q + 4, :].bitcast(I32), src[0, 4 * q : 4 * q + 4, :].bitcast(I32)
                )

        offs_l = load_list(offs, "offs_l")
        ca_l = load_list(ca, "ca_l")
        cb_l = load_list(cb, "cb_l")
        load_scale_rows(x_bytes, x_scales, range(QUADRANTS))
        load_scale_rows(w_bytes, w1_scales, range(1))
        x_sb = sb.tile([P, T], U32, name="x_sb", align_bytes=64)
        load_words(x_sb, x_words)
        load_scale_rows(w_bytes, w1_scales, range(1, QUADRANTS))
        w_words = shared.tile([P, H], U32, name="w_words", offset=C * WORD_BYTES // 2, align_bytes=64)
        load_words(w_words, w1_words)
        n1_l = load_list(n1, "n1_l")
        n2_l = load_list(n2, "n2_l")
        gs_sb = sb.tile([P, PACK], F32, name="gs_sb")
        nc.sync.dma_start(gs_sb[:], gs.rearrange("(p t) o -> p (t o)", t=PACK))
        n3_l = load_list(n3, "n3_l")
        n5_l = load_list(n5, "n5_l")
        n4_l = load_list(n4, "n4_l")
        n6_l = load_list(n6, "n6_l")

        def gather_bytes(lst, cols, name):
            got = sb.tile([P, cols], U8, name=name, align_bytes=64)
            nc.vector.tensor_copy(got[:], x_bytes[:].indirect(lst[:]))
            return got

        def deal_bytes(dealt, raw):
            nc.vector.tensor_copy(
                dealt[:].rearrange("p (t m) -> p t m", t=PACK), raw[:].rearrange("p (m t) -> p t m", t=PACK)
            )

        def gather_words_dealt(got, lst):
            nc.vector.tensor_copy(got[:].rearrange("p (t m) -> p m t", t=PACK), x_sb[:].indirect(lst[:]))

        def product(out, words, scales, t, rhs_words, rhs_scales):
            cols = slice(t * P, (t + 1) * P)
            nc.tensor.matmul_mx(
                out=out,
                lhsT=words[:, cols].bitcast(FP8X4),
                lhsT_scale=scales[:, cols],
                rhs=rhs_words.bitcast(FP8X4),
                rhs_scale=rhs_scales,
                start=True,
                stop=True,
            )

        def fetch(out, win, offsets, scale=1.0):
            nc.scalar.activation(out, win.indirect(offsets), COPY, scale=scale)

        def as_planes(planes):
            return planes.rearrange("p t (c i) -> p c t i", i=LINE)

        def as_words(rounded):
            return rounded.rearrange("p (c i) t -> p c t i", i=LINE)

        def quantise(words, scales, rounded):
            nc.vector.quantize_mx(out=words.bitcast(FP8X4), scales=scales, in_=rounded.rearrange("p j t -> p (j t)"))

        xq_scales = gather_bytes(offs_l, S, "xq_scales")
        ca_raw = gather_bytes(ca_l, C, "ca_raw")
        cb_raw = gather_bytes(cb_l, C, "cb_raw")
        xq_words = sb.tile([P, S], U32, name="xq_words", align_bytes=64)
        nc.vector.tensor_copy(xq_words[:], x_sb[:].indirect(offs_l[:]))
        w_scales = sb.tile([P, H], U8, name="w_scales", align_bytes=64)
        deal_bytes(w_scales, w_bytes)
        w_dealt = sb.tile([P, H], U32, name="w_dealt", align_bytes=64)
        nc.vector.tensor_copy(
            w_dealt[:].rearrange("p (t c i) -> p c t i", t=PACK, i=LINE),
            w_words[:].rearrange("p (c i t) -> p c t i", t=PACK, i=LINE),
        )

        y_ps = [ps.tile([P, S], F32, name="y_ps%d" % t, tag="bank%d" % t) for t in range(PACK)]
        for t in range(PACK):
            product(y_ps[t][:], w_dealt, w_scales, t, xq_words[:], xq_scales[:])

        ca_words = shared.tile([P, C], U32, name="ca_words", offset=0, align_bytes=64)
        cb_words = shared.tile([P, C], U32, name="cb_words", offset=C * WORD_BYTES, align_bytes=64)
        gather_words_dealt(ca_words, ca_l)
        gather_words_dealt(cb_words, cb_l)

        y_n1 = sb.tile([P, PACK, S], F32, name="y_n1")
        nc.scalar.activation(y_neg[:, plane(0)], y_ps[0][:], COPY, scale=-0.5)
        for t in range(PACK):
            if t < LAST:
                nc.scalar.activation(y_neg[:, plane(t + 1)], y_ps[t + 1][:], COPY, scale=-0.5)
            fetch(y_n1[:, t, :], y_neg[:, plane(t, 2)], n1_l[:], scale=-2.0)

        st_n2 = {
            (t, h): sb.tile([P, HALF], F32, name="st_n2_%d%d" % (t, h), tag="st_n2_%d%d" % (t, h), align_bytes=64)
            for t in range(1, PACK)
            for h in range(2)
        }
        own = sb.tile([P, LAST, S], F32, name="own")
        diff = sb.tile([P, S], F32, name="diff")
        z_f32 = sb.tile([P, PACK, S], F32, name="z_f32")
        z_bf = sb.tile([P, S, PACK], BF16, name="z_bf", align_bytes=64)
        z_words = sb.tile([P, S], U32, name="z_words", align_bytes=64)
        z_scales = sb.tile([P, S], U8, name="z_scales", align_bytes=64)

        def make_st(t):
            nc.vector.scalar_tensor_tensor(st[t][:, :S], y_neg[:, plane(t)], -2.0, y_n1[:, t, :], ALU.mult, ALU.max)

        def weight(t):
            return gs_sb[:, t : t + 1]

        make_st(0)
        nc.vector.tensor_tensor(diff[:], st[0][:].indirect(n2_l[:]), y_neg[:, plane(0)], ALU.add)
        for t in range(1, PACK):
            make_st(t)
        for t in range(1, PACK):
            nc.vector.tensor_scalar(own[:, t - 1, :], y_neg[:, plane(t)], weight(t), None, ALU.mult)
        nc.vector.tensor_scalar(z_f32[:, 0, :], diff[:], weight(0), None, ALU.mult)
        for h in range(2):
            for t in range(1, PACK):
                fetch(st_n2[t, h][:], st[t][:], half_list(n2_l, h))

        pair_scales = []
        for h, (raw, name) in enumerate(((ca_raw, "ca_scales"), (cb_raw, "cb_scales"))):
            cols = half_cols(h)
            for t in range(1, PACK):
                nc.vector.scalar_tensor_tensor(
                    z_f32[:, t, cols], st_n2[t, h][:], weight(t), own[:, t - 1, cols], ALU.mult, ALU.add
                )
            nc.vector.tensor_copy(as_words(z_bf[:, cols, :]), as_planes(z_f32[:, :, cols]))
            dealt = sb.tile([P, C], U8, name=name, tag="st_n2_%d%d" % (LAST, h), align_bytes=64)
            deal_bytes(dealt, raw)
            pair_scales.append(dealt)
            quantise(z_words[:, cols], z_scales[:, cols], z_bf[:, cols, :])
        ca_scales, cb_scales = pair_scales

        def a_leaves_psum(planes, h, bank):
            a_planes = a_sb[:, plane(0, PACK)].rearrange("p (t j) -> p t j", t=PACK)
            nc.scalar.activation(a_planes[:, planes, half_cols(h)], bank, COPY, scale=SIXTEENTH)

        z_half = [(z_words[:, half_cols(h)], z_scales[:, half_cols(h)]) for h in range(2)]
        first_a = ps.tile([P, PACK, HALF], F32, name="first_a", tag="bank0")
        for t in range(PACK):
            product(first_a[:, t, :], ca_words, ca_scales, t, *z_half[0])
        a_leaves_psum(slice(0, PACK), 0, first_a[:])

        second_a = [ps.tile([P, 2, HALF], F32, name="second_a%d" % u, tag="bank%d" % (u + 1)) for u in range(2)]
        b_ps = [ps.tile([P, S], F32, name="b_ps%d" % t, tag="bank%d" % (PACK + t)) for t in range(PACK)]
        for t in range(2):
            product(second_a[0][:, t, :], ca_words, ca_scales, t, *z_half[1])
        for t in range(PACK):
            product(b_ps[t][:], cb_words, cb_scales, t, z_words[:], z_scales[:])
        for t in range(2):
            product(second_a[1][:, t, :], ca_words, ca_scales, 2 + t, *z_half[1])

        a_got = sb.tile([P, PACK, 2, S], F32, name="a_got")
        sums = sb.tile([P, PACK, 2, S], F32, name="sums")
        o_f32 = sb.tile([P, PACK, S], F32, name="o_f32")
        o_bf = sb.tile([P, S, PACK], BF16, name="o_bf", align_bytes=64)
        o_words = sb.tile([P, S], U32, name="o_words", align_bytes=64)
        o_scales = sb.tile([P, S], U8, name="o_scales", align_bytes=64)
        b_got = sb.tile([P, 2, S], F32, name="b_got")
        out_rows = out_0.rearrange("(p t) j -> p t j", t=PACK)
        a_lists = (n3_l, n4_l)
        b_lists = (n5_l, n6_l)

        for t in range(PACK):
            nc.vector.tensor_scalar(b_sb[t][:, :S], b_ps[t][:], SIXTEENTH, None, ALU.mult)
        for t in range(PACK):
            if t < len(second_a):
                a_leaves_psum(slice(2 * t, 2 * t + 2), 1, second_a[t][:])
            for s in range(2):
                fetch(a_got[:, t, s, :], a_sb[:, plane(t, 2)], a_lists[s][:])
                if t == LAST:
                    fetch(b_got[:, s, :], b_sb[LAST][:], b_lists[s][:])

        def fetch_and_add(t, s):
            nc.vector.tensor_tensor(sums[:, t, s, :], b_sb[t][:].indirect(b_lists[s][:]), a_got[:, t, s, :], ALU.add)

        def add_last(s):
            nc.vector.tensor_tensor(sums[:, LAST, s, :], b_got[:, s, :], a_got[:, LAST, s, :], ALU.add)

        def finish(planes):
            nc.vector.tensor_tensor(o_f32[:, planes, :], sums[:, planes, 0, :], sums[:, planes, 1, :], ALU.max)
            nc.sync.dma_start(out_rows[:, planes, :], o_f32[:, planes, :])

        for t in range(2):
            for s in range(2):
                fetch_and_add(t, s)
        fetch_and_add(2, 0)
        finish(slice(0, 2))
        fetch_and_add(2, 1)
        add_last(0)
        finish(slice(2, LAST))
        add_last(1)
        finish(slice(LAST, PACK))

        nc.vector.tensor_copy(as_words(o_bf[:, :ON_VECTOR, :]), as_planes(o_f32[:, :, :ON_VECTOR]))
        nc.scalar.activation(as_words(o_bf[:, ON_VECTOR:, :]), as_planes(o_f32[:, :, ON_VECTOR:]), COPY)
        quantise(o_words[:], o_scales[:], o_bf[:])
        nc.sync.dma_start(out_1[0].rearrange("p n t -> p (n t)").bitcast(I32), o_words[:].bitcast(I32))
        for q in range(QUADRANTS):
            queue = nc.scalar if q % 2 == 0 else nc.sync
            queue.dma_start(out_2[0, 4 * q : 4 * q + 4, :].bitcast(I32), o_scales[32 * q : 32 * q + 4, :].bitcast(I32))
